import numpy as np
import ml_dtypes


def mxq(x, axis, fmt="e4m3"):
    dtype, down = {"e4m3": (ml_dtypes.float8_e4m3fn, 7), "e5m2": (ml_dtypes.float8_e5m2, 14)}[fmt]
    v = np.moveaxis(np.asarray(x, np.float32).astype(ml_dtypes.bfloat16).astype(np.float64), axis, -1)
    blocks = v.reshape(v.shape[:-1] + (-1, 32))
    amax = np.abs(blocks).max(-1, keepdims=True)
    byte = np.maximum(np.where(amax > 0, np.frexp(amax)[1] - 1 + 127, 0) - down, 1)
    scale = np.exp2(byte - 127.0)
    codes = (blocks / scale).astype(np.float32).astype(dtype).astype(np.float64)
    return np.moveaxis((codes * scale).reshape(v.shape), -1, axis)


WIDE = False


def mx_kscale(k):
    if not WIDE:
        return np.ones(k)
    levels = np.array([10, -10, 5, -5, 0])
    if k % 512:
        return np.exp2(np.random.permutation(np.resize(levels, k // 32))).repeat(32)
    a = np.empty((k // 512, 16))
    for p in range(k // 512):
        a[p, :8] = np.random.permutation(np.resize(levels, 8))
        for g in range(8):
            far = levels[np.abs(levels - a[p, g]) >= 10]
            a[p, g + 8] = far[np.random.randint(len(far))]
    return np.exp2(a.ravel()).repeat(32)


def f64(x):
    return np.asarray(x).astype(np.float64)


def striped(idx):
    return np.tile(np.asarray(idx).reshape(-1, 16).T, (8, 1)).astype(np.uint16)


def unstriped(offs):
    return offs[:16].T.reshape(-1).astype(np.int64)


E2M1 = np.array([0.0, 0.5, 1.0, 1.5, 2.0, 3.0, 4.0, 6.0, -0.0, -0.5, -1.0, -1.5, -2.0, -3.0, -4.0, -6.0])


def pack_weight(w, fmt):
    k, n = w.shape
    w = f64(np.asarray(w, np.float32).astype(ml_dtypes.bfloat16)).reshape(k // 32, 32, n)
    amax = np.abs(w).max(1)
    if fmt == "e4m3":
        byte = np.frexp(amax)[1] - 1 + 127 - 7
    else:
        mant, ex = np.frexp(amax / 6.0)
        byte = np.where(mant > 0.5, ex, ex - 1) + 127
    byte = np.clip(np.where(amax > 0, byte, 1), 1, 254)
    scaled = (w * np.exp2(127.0 - byte)[:, None, :]).reshape(k, n).astype(np.float32)
    by_word = np.ascontiguousarray(scaled.reshape(k // 512, 128, 4, n).transpose(0, 1, 3, 2))
    if fmt == "e4m3":
        words = by_word.astype(ml_dtypes.float8_e4m3fn).view(np.uint8)
    else:
        c = by_word.astype(ml_dtypes.float4_e2m1fn).view(np.uint8) & 0xF
        words = (c[..., 0::2] | (c[..., 1::2] << 4)).reshape(k // 512, 128, 2 * n)
    return np.ascontiguousarray(words), np.ascontiguousarray(byte.astype(np.uint8).reshape(k // 512, 16, n))


def unpack_weight(words, scales, fmt):
    g, _, n = scales.shape
    words = np.ascontiguousarray(words).reshape(g, 128, n, -1)
    if fmt == "e4m3":
        vals = words.view(ml_dtypes.float8_e4m3fn).astype(np.float64)
    else:
        nib = np.empty((g, 128, n, 4), np.uint8)
        nib[..., 0::2] = words & 0xF
        nib[..., 1::2] = words >> 4
        vals = E2M1[nib]
    vals = vals * np.repeat(np.exp2(scales.astype(np.float64) - 127.0), 8, axis=1)[..., None]
    return vals.transpose(0, 1, 3, 2).reshape(g * 512, n)


D, T, I, Q, G, E = 512, 2048, 512, 256, 32, 512


def setup_inputs():
    n = np.random.standard_normal
    idx = np.random.permutation(T)[:I]
    fd = mx_kscale(D)
    fi = mx_kscale(I)
    ti = np.ones(T)
    ti[idx] = fi
    keysp = pack_weight(n((D, T)) / fd[:, None], "e4m3")
    return {
        "query": (n((D, Q)) * 0.7 / np.sqrt(D) * fd[:, None]).astype(np.float32),
        "keys_words": keysp[0],
        "keys_scales": keysp[1],
        "reserve": (np.random.uniform(1.0, 8.0, (I, 1))).astype(np.float32),
        "us": (np.random.uniform(0.1, 0.4, (I, 1)) * fi[:, None]).astype(np.float32),
        "vals": (n((E, T)) / ti).astype(np.float32),
        "offs": striped(idx),
    }


def reference(query, keys_words, keys_scales, reserve, us, vals, offs):
    idx = unstriped(offs)
    keysu = unpack_weight(keys_words, keys_scales, "e4m3")
    keysidxg = keysu[:, idx]
    queryq = mxq(f64(query), 0, "e4m3")
    a = keysidxg.T @ queryq
    p = np.exp(a)
    b = f64(us) / (p.reshape(I, G, Q // G).sum(axis=2) + f64(reserve))
    br = np.repeat(b, Q // G, axis=1)
    w = p * br
    vt = f64(vals)[:, idx].T
    wq = mxq(w, 0, "e4m3")
    vtq = mxq(vt, 0, "e4m3")
    o = wq.T @ vtq
    return o

@@ -1,0 +1,199 @@
+from contextlib import ExitStack
+
+import concourse.mybir as mybir
+from concourse.masks import make_identity
+
+D, T, I, Q, G, E = 512, 2048, 512, 256, 32, 512
+P = 128
+PACK = 4
+TEAM = Q // G
+POOL_BYTES = 4 * T
+FLOPS = 2 * D * I * Q + 2 * I * Q * E
+
+F32 = mybir.dt.float32
+BF16 = mybir.dt.bfloat16
+I32 = mybir.dt.int32
+U32 = mybir.dt.uint32
+U16 = mybir.dt.uint16
+U8 = mybir.dt.uint8
+FP8X4 = mybir.dt.float8_e4m3fn_x4
+EXP = mybir.ActivationFunctionType.Exp
+MULT = mybir.AluOpType.mult
+
+
+def tile_attend_teamshares_kernel(tc, query, keys_words, keys_scales, reserve, us, vals, offs, out):
+    nc = tc.nc
+    halves = Q // P
+    members_half = TEAM // halves
+    with ExitStack() as ctx:
+        keep = ctx.enter_context(tc.tile_pool(name="keep", bufs=1))
+        shared = ctx.enter_context(tc.tile_pool(name="shared", bufs=1))
+        psum = ctx.enter_context(tc.psum_pool(name="psum", bufs=1))
+        psum2 = ctx.enter_context(tc.psum_pool(name="psum2", bufs=2))
+
+        key_scale_pool = keep.tile([P, T], U8, name="key_scale_pool", align_bytes=64)
+        nc.gpsimd.memset(key_scale_pool[:].bitcast(I32), 0)
+
+        offsets = keep.tile([P, I // 16], U16, name="offsets")
+        nc.sync.dma_start(offsets[:], offs)
+
+        query_raw = keep.tile([P, PACK, Q], F32, name="query_raw")
+        nc.sync.dma_start(query_raw[:], query.rearrange("(p j) q -> p j q", j=PACK))
+
+        for quad in range(4):
+            nc.sync.dma_start(
+                key_scale_pool[32 * quad : 32 * quad + 4, :].bitcast(I32),
+                keys_scales[0, 4 * quad : 4 * quad + 4, :].bitcast(I32),
+            )
+
+        key_pool = keep.tile([P, T], I32, name="key_pool", align_bytes=64)
+        nc.sync.dma_start(key_pool[:], keys_words[0].rearrange("p n t -> p (n t)").bitcast(I32))
+
+        val_pools = []
+        reserve_sb = keep.tile([P, PACK], F32, name="reserve_sb")
+        us_sb = keep.tile([P, PACK], F32, name="us_sb")
+        nc.sync.dma_start(reserve_sb[:], reserve.rearrange("(p t) o -> p (t o)", t=PACK))
+        nc.sync.dma_start(us_sb[:], us.rearrange("(p t) o -> p (t o)", t=PACK))
+        for k in range(E // P):
+            val_pool = shared.tile([P, T], F32, name="val_pool%d" % k, offset=k * POOL_BYTES, align_bytes=64)
+            nc.sync.dma_start(val_pool[:], vals[k * P : (k + 1) * P, :])
+            val_pools.append(val_pool)
+
+        ident = keep.tile([P, P], F32, name="ident")
+        make_identity(nc, ident[:])
+
+        query_bf = keep.tile([P, Q, PACK], BF16, name="query_bf", align_bytes=64)
+        query_codes = keep.tile([P, Q], U32, name="query_codes", align_bytes=64)
+        query_scales = keep.tile([P, Q], U8, name="query_scales", align_bytes=64)
+        for h in range(halves):
+            members = slice(h * members_half, (h + 1) * members_half)
+            nc.scalar.copy(
+                query_bf[:].rearrange("p (r g) j -> p g j r", r=TEAM)[:, :, :, members],
+                query_raw[:].rearrange("p j (g r) -> p g j r", r=TEAM)[:, :, :, members],
+            )
+        nc.vector.quantize_mx(
+            out=query_codes[:].bitcast(FP8X4),
+            scales=query_scales[:],
+            in_=query_bf[:].rearrange("p q j -> p (q j)"),
+        )
+
+        key_scale_listed = keep.tile([P, I], U8, name="key_scale_listed", align_bytes=64)
+        nc.vector.tensor_copy(key_scale_listed[:], key_scale_pool[:].indirect(offsets[:]))
+        key_scales = keep.tile([P, PACK, P], U8, name="key_scales", align_bytes=64)
+        nc.vector.tensor_copy(key_scales[:], key_scale_listed[:].rearrange("p (s t) -> p t s", t=PACK))
+        key_codes = keep.tile([P, PACK, P], U32, name="key_codes", align_bytes=64)
+        nc.vector.tensor_copy(
+            key_codes[:].rearrange("p t s -> p s t"), key_pool[:].bitcast(U32).indirect(offsets[:])
+        )
+
+        reserve_wide = keep.tile([P, G, PACK], F32, name="reserve_wide")
+        nc.scalar.copy(reserve_wide[:], reserve_sb[:].unsqueeze(1).to_broadcast([P, G, PACK]))
+
+        expd = keep.tile([P, TEAM, G, PACK], F32, name="expd", tag="slot3", align_bytes=64)
+        for h in range(halves):
+            scores = psum.tile([P, PACK, P], F32, name="scores%d" % h)
+            for t in range(PACK):
+                nc.tensor.matmul_mx(
+                    out=scores[:, t, :],
+                    lhsT=key_codes[:, t, :].bitcast(FP8X4),
+                    lhsT_scale=key_scales[:, t, :],
+                    rhs=query_codes[:, h * P : (h + 1) * P].bitcast(FP8X4),
+                    rhs_scale=query_scales[:, h * P : (h + 1) * P],
+                    start=True,
+                    stop=True,
+                )
+            nc.scalar.activation(
+                expd[:, h * members_half : (h + 1) * members_half, :, :],
+                scores[:].rearrange("p t (r g) -> p r g t", g=G),
+                EXP,
+            )
+
+        denom_t = psum.tile([P, P], F32, name="denom_t")
+        nc.tensor.matmul(
+            denom_t[:], reserve_wide[:].rearrange("p g t -> p (g t)"), ident[:],
+            start=True, stop=False, is_transpose=True,
+        )
+        for r in range(TEAM):
+            nc.tensor.matmul(
+                denom_t[:], expd[:, r, :, :].rearrange("p g t -> p (g t)"), ident[:],
+                start=False, stop=(r == TEAM - 1), is_transpose=True,
+            )
+        listed = {}
+        vt_bf = {}
+        vt_mx = {}
+        out_view = out.rearrange("(h p) e -> p h e", p=P)
+
+        def gather_values(k):
+            listed[k] = keep.tile([P, I], BF16, name="listed%d" % k, tag="slot%d" % k, align_bytes=64)
+            nc.vector.tensor_copy(listed[k][:], val_pools[k][:].indirect(offsets[:]))
+
+        def turn_values(k):
+            pairs = listed[k][:].bitcast(F32)
+            turned = psum2.tile([P, 2, P], F32, name="turned")
+            for u in range(2):
+                nc.tensor.transpose(turned[:, u, :], pairs[:, u : I // 2 : 2], ident[:])
+            vt_bf[k] = keep.tile([P, P * PACK], BF16, name="vt_bf%d" % k, align_bytes=64)
+            nc.scalar.copy(
+                vt_bf[k][:].bitcast(F32).rearrange("p (e u) -> p e u", u=2),
+                turned[:].rearrange("p u e -> p e u"),
+            )
+
+        def quantise_values(k, after):
+            vt_codes = shared.tile(
+                [P, P], U32, name="vt_codes%d" % k, offset=after * POOL_BYTES + 1024 + 512 * k, align_bytes=64
+            )
+            vt_scales = keep.tile([P, P], U8, name="vt_scales%d" % k, align_bytes=64)
+            nc.vector.quantize_mx(out=vt_codes[:].bitcast(FP8X4), scales=vt_scales[:], in_=vt_bf[k][:])
+            vt_mx[k] = (vt_codes, vt_scales)
+
+        def multiply_and_store(k):
+            vt_codes, vt_scales = vt_mx[k]
+            acc = psum2.tile([P, halves, P], F32, name="acc")
+            for h in range(halves):
+                nc.tensor.matmul_mx(
+                    out=acc[:, h, :],
+                    lhsT=w_codes[:, h * P : (h + 1) * P].bitcast(FP8X4),
+                    lhsT_scale=w_scales[:, h * P : (h + 1) * P],
+                    rhs=vt_codes[:].bitcast(FP8X4),
+                    rhs_scale=vt_scales[:],
+                    start=True,
+                    stop=True,
+                )
+            result = keep.tile([P, halves, P], F32, name="result%d" % k)
+            nc.scalar.copy(result[:], acc[:])
+            nc.sync.dma_start(out_view[:, :, k * P : (k + 1) * P], result[:])
+
+        gather_values(0)
+        turn_values(0)
+        gather_values(1)
+        recip_t = shared.tile([P, P], F32, name="recip_t", offset=POOL_BYTES, align_bytes=64)
+        nc.vector.reciprocal(recip_t[:], denom_t[:])
+        turn_values(1)
+        recip = psum.tile([P, G, PACK], F32, name="recip")
+        nc.tensor.transpose(recip[:].rearrange("p g t -> p (g t)"), recip_t[:], ident[:])
+        gather_values(2)
+        turn_values(2)
+        share = shared.tile([P, G, PACK], F32, name="share", offset=2 * POOL_BYTES, align_bytes=64)
+        nc.vector.tensor_tensor(share[:], recip[:], us_sb[:].unsqueeze(1).to_broadcast([P, G, PACK]), MULT)
+        quantise_values(0, 2)
+
+        w_bf = keep.tile([P, G, TEAM, PACK], BF16, name="w_bf", align_bytes=64)
+        nc.vector.tensor_tensor(
+            w_bf[:],
+            expd[:].rearrange("p r g t -> p g r t"),
+            share[:].unsqueeze(2).to_broadcast([P, G, TEAM, PACK]),
+            MULT,
+        )
+        gather_values(3)
+        turn_values(3)
+        w_codes = shared.tile([P, Q], U32, name="w_codes", offset=3 * POOL_BYTES, align_bytes=64)
+        w_scales = keep.tile([P, Q], U8, name="w_scales", align_bytes=64)
+        nc.vector.quantize_mx(
+            out=w_codes[:].bitcast(FP8X4),
+            scales=w_scales[:],
+            in_=w_bf[:].rearrange("p g r t -> p (g r t)"),
+        )
+        multiply_and_store(0)
+        for k in (1, 2, 3):
+            quantise_values(k, 3)
+            multiply_and_store(k)

@@ -8,6 +8,7 @@ P = 128
 PACK = 4
 TEAM = Q // G
 POOL_BYTES = 4 * T
+SCALAR_TILE = 2
 FLOPS = 2 * D * I * Q + 2 * I * Q * E
 
 F32 = mybir.dt.float32
@@ -18,6 +19,7 @@ U16 = mybir.dt.uint16
 U8 = mybir.dt.uint8
 FP8X4 = mybir.dt.float8_e4m3fn_x4
 EXP = mybir.ActivationFunctionType.Exp
+COPY = mybir.ActivationFunctionType.Copy
 MULT = mybir.AluOpType.mult
 
 
@@ -46,18 +48,31 @@ def tile_attend_teamshares_kernel(tc, query, keys_words, keys_scales, reserve, u
                 keys_scales[0, 4 * quad : 4 * quad + 4, :].bitcast(I32),
             )
 
+        reserve_sb = keep.tile([P, PACK], F32, name="reserve_sb")
+        nc.sync.dma_start(reserve_sb[:], reserve.rearrange("(p t) o -> p (t o)", t=PACK))
+
         key_pool = keep.tile([P, T], I32, name="key_pool", align_bytes=64)
         nc.sync.dma_start(key_pool[:], keys_words[0].rearrange("p n t -> p (n t)").bitcast(I32))
 
         val_pools = []
-        reserve_sb = keep.tile([P, PACK], F32, name="reserve_sb")
         us_sb = keep.tile([P, PACK], F32, name="us_sb")
-        nc.sync.dma_start(reserve_sb[:], reserve.rearrange("(p t) o -> p (t o)", t=PACK))
         nc.sync.dma_start(us_sb[:], us.rearrange("(p t) o -> p (t o)", t=PACK))
         for k in range(E // P):
-            val_pool = shared.tile([P, T], F32, name="val_pool%d" % k, offset=k * POOL_BYTES, align_bytes=64)
-            nc.sync.dma_start(val_pool[:], vals[k * P : (k + 1) * P, :])
-            val_pools.append(val_pool)
+            rows = vals[k * P : (k + 1) * P, :]
+            if k == SCALAR_TILE:
+                parts = []
+                for c in range(2):
+                    part = shared.tile(
+                        [P, T // 2], F32, name="val_part%d" % c,
+                        offset=k * POOL_BYTES + c * POOL_BYTES // 2, align_bytes=64,
+                    )
+                    nc.sync.dma_start(part[:], rows[:, c * T // 2 : (c + 1) * T // 2])
+                    parts.append(part)
+                val_pools.append(parts)
+            else:
+                val_pool = shared.tile([P, T], F32, name="val_pool%d" % k, offset=k * POOL_BYTES, align_bytes=64)
+                nc.sync.dma_start(val_pool[:], rows)
+                val_pools.append(val_pool)
 
         ident = keep.tile([P, P], F32, name="ident")
         make_identity(nc, ident[:])
@@ -118,64 +133,73 @@ def tile_attend_teamshares_kernel(tc, query, keys_words, keys_scales, reserve, u
                 denom_t[:], expd[:, r, :, :].rearrange("p g t -> p (g t)"), ident[:],
                 start=False, stop=(r == TEAM - 1), is_transpose=True,
             )
-        listed = {}
-        vt_bf = {}
-        vt_mx = {}
         out_view = out.rearrange("(h p) e -> p h e", p=P)
+        listed = {}
 
-        def gather_values(k):
+        def gather_on_vector(k):
             listed[k] = keep.tile([P, I], BF16, name="listed%d" % k, tag="slot%d" % k, align_bytes=64)
             nc.vector.tensor_copy(listed[k][:], val_pools[k][:].indirect(offsets[:]))
 
-        def turn_values(k):
+        def gather_on_scalar(k):
+            rounded = keep.tile([P, T], BF16, name="rounded%d" % k, align_bytes=64)
+            for c in range(2):
+                nc.scalar.activation(rounded[:, c * T // 2 : (c + 1) * T // 2], val_pools[k][c][:], COPY)
+            listed[k] = keep.tile([P, I], BF16, name="listed%d" % k, align_bytes=64)
+            nc.scalar.activation(listed[k][:], rounded[:].indirect(offsets[:]), COPY)
+
+        def turn_values(k, vt_bf):
             pairs = listed[k][:].bitcast(F32)
             turned = psum2.tile([P, 2, P], F32, name="turned")
             for u in range(2):
                 nc.tensor.transpose(turned[:, u, :], pairs[:, u : I // 2 : 2], ident[:])
-            vt_bf[k] = keep.tile([P, P * PACK], BF16, name="vt_bf%d" % k, align_bytes=64)
             nc.scalar.copy(
-                vt_bf[k][:].bitcast(F32).rearrange("p (e u) -> p e u", u=2),
+                vt_bf.bitcast(F32).rearrange("p (e u) -> p e u", u=2),
                 turned[:].rearrange("p u e -> p e u"),
             )
 
-        def quantise_values(k, after):
-            vt_codes = shared.tile(
-                [P, P], U32, name="vt_codes%d" % k, offset=after * POOL_BYTES + 1024 + 512 * k, align_bytes=64
+        def quantise_values(vt_bf, vt_codes, name):
+            vt_scales = keep.tile(list(vt_codes.shape), U8, name=name, align_bytes=64)
+            nc.vector.quantize_mx(out=vt_codes[:].bitcast(FP8X4), scales=vt_scales[:], in_=vt_bf[:])
+            return vt_scales
+
+        def multiply(acc, h, vt_codes, vt_scales):
+            nc.tensor.matmul_mx(
+                out=acc,
+                lhsT=w_codes[:, h * P : (h + 1) * P].bitcast(FP8X4),
+                lhsT_scale=w_scales[:, h * P : (h + 1) * P],
+                rhs=vt_codes[:].bitcast(FP8X4),
+                rhs_scale=vt_scales[:],
+                start=True,
+                stop=True,
             )
-            vt_scales = keep.tile([P, P], U8, name="vt_scales%d" % k, align_bytes=64)
-            nc.vector.quantize_mx(out=vt_codes[:].bitcast(FP8X4), scales=vt_scales[:], in_=vt_bf[k][:])
-            vt_mx[k] = (vt_codes, vt_scales)
 
-        def multiply_and_store(k):
-            vt_codes, vt_scales = vt_mx[k]
-            acc = psum2.tile([P, halves, P], F32, name="acc")
+        def multiply_and_store(first, vt_codes, vt_scales):
+            width = vt_codes.shape[1]
+            acc = psum2.tile([P, halves, width], F32, name="acc")
             for h in range(halves):
-                nc.tensor.matmul_mx(
-                    out=acc[:, h, :],
-                    lhsT=w_codes[:, h * P : (h + 1) * P].bitcast(FP8X4),
-                    lhsT_scale=w_scales[:, h * P : (h + 1) * P],
-                    rhs=vt_codes[:].bitcast(FP8X4),
-                    rhs_scale=vt_scales[:],
-                    start=True,
-                    stop=True,
-                )
-            result = keep.tile([P, halves, P], F32, name="result%d" % k)
+                multiply(acc[:, h, :], h, vt_codes, vt_scales)
+            result = keep.tile([P, halves, width], F32, name="result%d" % first)
             nc.scalar.copy(result[:], acc[:])
-            nc.sync.dma_start(out_view[:, :, k * P : (k + 1) * P], result[:])
+            nc.sync.dma_start(out_view[:, :, first * P : first * P + width], result[:])
 
-        gather_values(0)
-        turn_values(0)
-        gather_values(1)
-        recip_t = shared.tile([P, P], F32, name="recip_t", offset=POOL_BYTES, align_bytes=64)
+        vt_first = keep.tile([P, P * PACK], BF16, name="vt_first", align_bytes=64)
+        vt_middle = shared.tile(
+            [P, 2 * P * PACK], BF16, name="vt_middle", offset=2 * POOL_BYTES + POOL_BYTES // 2, align_bytes=64
+        )
+        vt_last = keep.tile([P, P * PACK], BF16, name="vt_last", align_bytes=64)
+
+        gather_on_vector(0)
+        recip_t = shared.tile([P, P], F32, name="recip_t", offset=0, align_bytes=64)
         nc.vector.reciprocal(recip_t[:], denom_t[:])
-        turn_values(1)
+        turn_values(0, vt_first[:])
         recip = psum.tile([P, G, PACK], F32, name="recip")
         nc.tensor.transpose(recip[:].rearrange("p g t -> p (g t)"), recip_t[:], ident[:])
-        gather_values(2)
-        turn_values(2)
-        share = shared.tile([P, G, PACK], F32, name="share", offset=2 * POOL_BYTES, align_bytes=64)
+        gather_on_vector(1)
+        share = shared.tile([P, G, PACK], F32, name="share", offset=POOL_BYTES, align_bytes=64)
         nc.vector.tensor_tensor(share[:], recip[:], us_sb[:].unsqueeze(1).to_broadcast([P, G, PACK]), MULT)
-        quantise_values(0, 2)
+        first_codes = shared.tile([P, P], U32, name="first_codes", offset=POOL_BYTES + 1024, align_bytes=64)
+        first_scales = quantise_values(vt_first, first_codes, "first_scales")
+        gather_on_scalar(2)
 
         w_bf = keep.tile([P, G, TEAM, PACK], BF16, name="w_bf", align_bytes=64)
         nc.vector.tensor_tensor(
@@ -184,8 +208,10 @@ def tile_attend_teamshares_kernel(tc, query, keys_words, keys_scales, reserve, u
             share[:].unsqueeze(2).to_broadcast([P, G, TEAM, PACK]),
             MULT,
         )
-        gather_values(3)
-        turn_values(3)
+        turn_values(1, vt_middle[:, : P * PACK])
+        turn_values(2, vt_middle[:, P * PACK :])
+        gather_on_vector(3)
+        turn_values(3, vt_last[:])
         w_codes = shared.tile([P, Q], U32, name="w_codes", offset=3 * POOL_BYTES, align_bytes=64)
         w_scales = keep.tile([P, Q], U8, name="w_scales", align_bytes=64)
         nc.vector.quantize_mx(
@@ -193,7 +219,20 @@ def tile_attend_teamshares_kernel(tc, query, keys_words, keys_scales, reserve, u
             scales=w_scales[:],
             in_=w_bf[:].rearrange("p g r t -> p (g r t)"),
         )
-        multiply_and_store(0)
-        for k in (1, 2, 3):
-            quantise_values(k, 3)
-            multiply_and_store(k)
+        middle_codes = shared.tile(
+            [P, 2 * P], U32, name="middle_codes", offset=3 * POOL_BYTES + 4 * Q, align_bytes=64
+        )
+        middle_scales = quantise_values(vt_middle, middle_codes, "middle_scales")
+        last_codes = keep.tile([P, P], U32, name="last_codes", align_bytes=64)
+        last_scales = quantise_values(vt_last, last_codes, "last_scales")
+        multiply_and_store(0, first_codes, first_scales)
+        multiply_and_store(1, middle_codes, middle_scales)
+
+        for h, (engine_copy, queue) in enumerate(
+            ((nc.vector.tensor_copy, nc.sync), (nc.scalar.copy, nc.scalar))
+        ):
+            acc = psum.tile([P, P], F32, name="last_acc%d" % h, tag="scores%d" % h)
+            multiply(acc[:], h, last_codes, last_scales)
+            result = keep.tile([P, P], F32, name="last_result%d" % h)
+            engine_copy(result[:], acc[:])
+            queue.dma_start(out[h * P : (h + 1) * P, 3 * P :], result[:])

from contextlib import ExitStack

import concourse.mybir as mybir
from concourse.masks import make_identity

D, T, I, Q, G, E = 512, 2048, 512, 256, 32, 512
P = 128
PACK = 4
TEAM = Q // G
POOL_BYTES = 4 * T
SCALAR_TILE = 2
FLOPS = 2 * D * I * Q + 2 * I * Q * E

F32 = mybir.dt.float32
BF16 = mybir.dt.bfloat16
I32 = mybir.dt.int32
U32 = mybir.dt.uint32
U16 = mybir.dt.uint16
U8 = mybir.dt.uint8
FP8X4 = mybir.dt.float8_e4m3fn_x4
EXP = mybir.ActivationFunctionType.Exp
COPY = mybir.ActivationFunctionType.Copy
MULT = mybir.AluOpType.mult


def tile_attend_teamshares_kernel(tc, query, keys_words, keys_scales, reserve, us, vals, offs, out):
    nc = tc.nc
    halves = Q // P
    members_half = TEAM // halves
    with ExitStack() as ctx:
        keep = ctx.enter_context(tc.tile_pool(name="keep", bufs=1))
        shared = ctx.enter_context(tc.tile_pool(name="shared", bufs=1))
        psum = ctx.enter_context(tc.psum_pool(name="psum", bufs=1))
        psum2 = ctx.enter_context(tc.psum_pool(name="psum2", bufs=2))

        key_scale_pool = keep.tile([P, T], U8, name="key_scale_pool", align_bytes=64)
        nc.gpsimd.memset(key_scale_pool[:].bitcast(I32), 0)

        offsets = keep.tile([P, I // 16], U16, name="offsets")
        nc.sync.dma_start(offsets[:], offs)

        query_raw = keep.tile([P, PACK, Q], F32, name="query_raw")
        nc.sync.dma_start(query_raw[:], query.rearrange("(p j) q -> p j q", j=PACK))

        for quad in range(4):
            nc.sync.dma_start(
                key_scale_pool[32 * quad : 32 * quad + 4, :].bitcast(I32),
                keys_scales[0, 4 * quad : 4 * quad + 4, :].bitcast(I32),
            )

        reserve_sb = keep.tile([P, PACK], F32, name="reserve_sb")
        nc.sync.dma_start(reserve_sb[:], reserve.rearrange("(p t) o -> p (t o)", t=PACK))

        key_pool = keep.tile([P, T], I32, name="key_pool", align_bytes=64)
        nc.sync.dma_start(key_pool[:], keys_words[0].rearrange("p n t -> p (n t)").bitcast(I32))

        val_pools = []
        us_sb = keep.tile([P, PACK], F32, name="us_sb")
        nc.sync.dma_start(us_sb[:], us.rearrange("(p t) o -> p (t o)", t=PACK))
        for k in range(E // P):
            rows = vals[k * P : (k + 1) * P, :]
            if k == SCALAR_TILE:
                parts = []
                for c in range(2):
                    part = shared.tile(
                        [P, T // 2], F32, name="val_part%d" % c,
                        offset=k * POOL_BYTES + c * POOL_BYTES // 2, align_bytes=64,
                    )
                    nc.sync.dma_start(part[:], rows[:, c * T // 2 : (c + 1) * T // 2])
                    parts.append(part)
                val_pools.append(parts)
            else:
                val_pool = shared.tile([P, T], F32, name="val_pool%d" % k, offset=k * POOL_BYTES, align_bytes=64)
                nc.sync.dma_start(val_pool[:], rows)
                val_pools.append(val_pool)

        ident = keep.tile([P, P], F32, name="ident")
        make_identity(nc, ident[:])

        query_bf = keep.tile([P, Q, PACK], BF16, name="query_bf", align_bytes=64)
        query_codes = keep.tile([P, Q], U32, name="query_codes", align_bytes=64)
        query_scales = keep.tile([P, Q], U8, name="query_scales", align_bytes=64)
        for h in range(halves):
            members = slice(h * members_half, (h + 1) * members_half)
            nc.scalar.copy(
                query_bf[:].rearrange("p (r g) j -> p g j r", r=TEAM)[:, :, :, members],
                query_raw[:].rearrange("p j (g r) -> p g j r", r=TEAM)[:, :, :, members],
            )
        nc.vector.quantize_mx(
            out=query_codes[:].bitcast(FP8X4),
            scales=query_scales[:],
            in_=query_bf[:].rearrange("p q j -> p (q j)"),
        )

        key_scale_listed = keep.tile([P, I], U8, name="key_scale_listed", align_bytes=64)
        nc.vector.tensor_copy(key_scale_listed[:], key_scale_pool[:].indirect(offsets[:]))
        key_scales = keep.tile([P, PACK, P], U8, name="key_scales", align_bytes=64)
        nc.vector.tensor_copy(key_scales[:], key_scale_listed[:].rearrange("p (s t) -> p t s", t=PACK))
        key_codes = keep.tile([P, PACK, P], U32, name="key_codes", align_bytes=64)
        nc.vector.tensor_copy(
            key_codes[:].rearrange("p t s -> p s t"), key_pool[:].bitcast(U32).indirect(offsets[:])
        )

        reserve_wide = keep.tile([P, G, PACK], F32, name="reserve_wide")
        nc.scalar.copy(reserve_wide[:], reserve_sb[:].unsqueeze(1).to_broadcast([P, G, PACK]))

        expd = keep.tile([P, TEAM, G, PACK], F32, name="expd", tag="slot3", align_bytes=64)
        for h in range(halves):
            scores = psum.tile([P, PACK, P], F32, name="scores%d" % h)
            for t in range(PACK):
                nc.tensor.matmul_mx(
                    out=scores[:, t, :],
                    lhsT=key_codes[:, t, :].bitcast(FP8X4),
                    lhsT_scale=key_scales[:, t, :],
                    rhs=query_codes[:, h * P : (h + 1) * P].bitcast(FP8X4),
                    rhs_scale=query_scales[:, h * P : (h + 1) * P],
                    start=True,
                    stop=True,
                )
            nc.scalar.activation(
                expd[:, h * members_half : (h + 1) * members_half, :, :],
                scores[:].rearrange("p t (r g) -> p r g t", g=G),
                EXP,
            )

        denom_t = psum.tile([P, P], F32, name="denom_t")
        nc.tensor.matmul(
            denom_t[:], reserve_wide[:].rearrange("p g t -> p (g t)"), ident[:],
            start=True, stop=False, is_transpose=True,
        )
        for r in range(TEAM):
            nc.tensor.matmul(
                denom_t[:], expd[:, r, :, :].rearrange("p g t -> p (g t)"), ident[:],
                start=False, stop=(r == TEAM - 1), is_transpose=True,
            )
        out_view = out.rearrange("(h p) e -> p h e", p=P)
        listed = {}

        def gather_on_vector(k):
            listed[k] = keep.tile([P, I], BF16, name="listed%d" % k, tag="slot%d" % k, align_bytes=64)
            nc.vector.tensor_copy(listed[k][:], val_pools[k][:].indirect(offsets[:]))

        def gather_on_scalar(k):
            rounded = keep.tile([P, T], BF16, name="rounded%d" % k, align_bytes=64)
            for c in range(2):
                nc.scalar.activation(rounded[:, c * T // 2 : (c + 1) * T // 2], val_pools[k][c][:], COPY)
            listed[k] = keep.tile([P, I], BF16, name="listed%d" % k, align_bytes=64)
            nc.scalar.activation(listed[k][:], rounded[:].indirect(offsets[:]), COPY)

        def turn_values(k, vt_bf):
            pairs = listed[k][:].bitcast(F32)
            turned = psum2.tile([P, 2, P], F32, name="turned")
            for u in range(2):
                nc.tensor.transpose(turned[:, u, :], pairs[:, u : I // 2 : 2], ident[:])
            nc.scalar.copy(
                vt_bf.bitcast(F32).rearrange("p (e u) -> p e u", u=2),
                turned[:].rearrange("p u e -> p e u"),
            )

        def quantise_values(vt_bf, vt_codes, name):
            vt_scales = keep.tile(list(vt_codes.shape), U8, name=name, align_bytes=64)
            nc.vector.quantize_mx(out=vt_codes[:].bitcast(FP8X4), scales=vt_scales[:], in_=vt_bf[:])
            return vt_scales

        def multiply(acc, h, vt_codes, vt_scales):
            nc.tensor.matmul_mx(
                out=acc,
                lhsT=w_codes[:, h * P : (h + 1) * P].bitcast(FP8X4),
                lhsT_scale=w_scales[:, h * P : (h + 1) * P],
                rhs=vt_codes[:].bitcast(FP8X4),
                rhs_scale=vt_scales[:],
                start=True,
                stop=True,
            )

        def multiply_and_store(first, vt_codes, vt_scales):
            width = vt_codes.shape[1]
            acc = psum2.tile([P, halves, width], F32, name="acc")
            for h in range(halves):
                multiply(acc[:, h, :], h, vt_codes, vt_scales)
            result = keep.tile([P, halves, width], F32, name="result%d" % first)
            nc.scalar.copy(result[:], acc[:])
            nc.sync.dma_start(out_view[:, :, first * P : first * P + width], result[:])

        vt_first = keep.tile([P, P * PACK], BF16, name="vt_first", align_bytes=64)
        vt_middle = shared.tile(
            [P, 2 * P * PACK], BF16, name="vt_middle", offset=2 * POOL_BYTES + POOL_BYTES // 2, align_bytes=64
        )
        vt_last = keep.tile([P, P * PACK], BF16, name="vt_last", align_bytes=64)

        gather_on_vector(0)
        recip_t = shared.tile([P, P], F32, name="recip_t", offset=0, align_bytes=64)
        nc.vector.reciprocal(recip_t[:], denom_t[:])
        turn_values(0, vt_first[:])
        recip = psum.tile([P, G, PACK], F32, name="recip")
        nc.tensor.transpose(recip[:].rearrange("p g t -> p (g t)"), recip_t[:], ident[:])
        gather_on_vector(1)
        share = shared.tile([P, G, PACK], F32, name="share", offset=POOL_BYTES, align_bytes=64)
        nc.vector.tensor_tensor(share[:], recip[:], us_sb[:].unsqueeze(1).to_broadcast([P, G, PACK]), MULT)
        first_codes = shared.tile([P, P], U32, name="first_codes", offset=POOL_BYTES + 1024, align_bytes=64)
        first_scales = quantise_values(vt_first, first_codes, "first_scales")
        gather_on_scalar(2)

        w_bf = keep.tile([P, G, TEAM, PACK], BF16, name="w_bf", align_bytes=64)
        nc.vector.tensor_tensor(
            w_bf[:],
            expd[:].rearrange("p r g t -> p g r t"),
            share[:].unsqueeze(2).to_broadcast([P, G, TEAM, PACK]),
            MULT,
        )
        turn_values(1, vt_middle[:, : P * PACK])
        turn_values(2, vt_middle[:, P * PACK :])
        gather_on_vector(3)
        turn_values(3, vt_last[:])
        w_codes = shared.tile([P, Q], U32, name="w_codes", offset=3 * POOL_BYTES, align_bytes=64)
        w_scales = keep.tile([P, Q], U8, name="w_scales", align_bytes=64)
        nc.vector.quantize_mx(
            out=w_codes[:].bitcast(FP8X4),
            scales=w_scales[:],
            in_=w_bf[:].rearrange("p g r t -> p (g r t)"),
        )
        middle_codes = shared.tile(
            [P, 2 * P], U32, name="middle_codes", offset=3 * POOL_BYTES + 4 * Q, align_bytes=64
        )
        middle_scales = quantise_values(vt_middle, middle_codes, "middle_scales")
        last_codes = keep.tile([P, P], U32, name="last_codes", align_bytes=64)
        last_scales = quantise_values(vt_last, last_codes, "last_scales")
        multiply_and_store(0, first_codes, first_scales)
        multiply_and_store(1, middle_codes, middle_scales)

        for h, (engine_copy, queue) in enumerate(
            ((nc.vector.tensor_copy, nc.sync), (nc.scalar.copy, nc.scalar))
        ):
            acc = psum.tile([P, P], F32, name="last_acc%d" % h, tag="scores%d" % h)
            multiply(acc[:], h, last_codes, last_scales)
            result = keep.tile([P, P], F32, name="last_result%d" % h)
            engine_copy(result[:], acc[:])
            queue.dma_start(out[h * P : (h + 1) * P, 3 * P :], result[:])
